import numpy as np
import ml_dtypes


def mxq(x, axis, fmt="e4m3"):
    dtype, down = {"e4m3": (ml_dtypes.float8_e4m3fn, 7), "e5m2": (ml_dtypes.float8_e5m2, 14)}[fmt]
    v = np.moveaxis(np.asarray(x, np.float32).astype(ml_dtypes.bfloat16).astype(np.float64), axis, -1)
    blocks = v.reshape(v.shape[:-1] + (-1, 32))
    amax = np.abs(blocks).max(-1, keepdims=True)
    byte = np.maximum(np.where(amax > 0, np.frexp(amax)[1] - 1 + 127, 0) - down, 1)
    scale = np.exp2(byte - 127.0)
    codes = (blocks / scale).astype(np.float32).astype(dtype).astype(np.float64)
    return np.moveaxis((codes * scale).reshape(v.shape), -1, axis)


WIDE = False


def mx_kscale(k):
    if not WIDE:
        return np.ones(k)
    levels = np.array([10, -10, 5, -5, 0])
    if k % 512:
        return np.exp2(np.random.permutation(np.resize(levels, k // 32))).repeat(32)
    a = np.empty((k // 512, 16))
    for p in range(k // 512):
        a[p, :8] = np.random.permutation(np.resize(levels, 8))
        for g in range(8):
            far = levels[np.abs(levels - a[p, g]) >= 10]
            a[p, g + 8] = far[np.random.randint(len(far))]
    return np.exp2(a.ravel()).repeat(32)


def f64(x):
    return np.asarray(x).astype(np.float64)


def striped(idx):
    return np.tile(idx.reshape(-1, 16).T, (8, 1)).astype(np.uint16)


def unstriped(offs):
    return offs[:16].T.reshape(-1).astype(np.int64)


K, T, S, N = 512, 2048, 1024, 256


def setup_inputs():
    n = np.random.standard_normal
    s = mx_kscale(K)[:, None]
    return {
        "xT": (n((K, S)) * s).astype(np.float32),
        "w": (n((K, N)) / np.sqrt(K) / s).astype(np.float32),
        "b": (0.3 * n((N, 1))).astype(np.float32),
        "gate": np.tile(np.random.uniform(0.2, 1.0, S), (N, 1)).astype(np.float32),
        "offs": striped(np.sort(np.random.permutation(T)[:S])),
    }


def reference(xT, w, b, gate, offs):
    idx = unstriped(offs)
    xq = mxq(f64(xT), 0, "e4m3")
    y = mxq(f64(w), 0, "e4m3").T @ xq
    y = y + f64(b)
    out = np.zeros((N, T))
    out[:, idx] = f64(gate) * y
    return out

@@ -1,0 +1,139 @@
+from contextlib import ExitStack
+
+import concourse.mybir as mybir
+
+K, T, S, N = 512, 2048, 1024, 256
+FLOPS = 2 * K * N * S
+BYTES = 4 * (K * S + K * N + N + S + N * T) + 2 * 128 * (S // 16)
+
+F32 = mybir.dt.float32
+BF16 = mybir.dt.bfloat16
+U32 = mybir.dt.uint32
+U16 = mybir.dt.uint16
+U8 = mybir.dt.uint8
+FP8X4 = mybir.dt.float8_e4m3fn_x4
+
+P = 128
+PACK = 4
+PIECE = 256
+PIECES = S // PIECE
+M_TILES = N // P
+LIST_COLS = PIECE // 16
+
+
+def interleave(copy, grouped, raw, first, last):
+    if first == last:
+        return
+    copy(
+        out=grouped[:, PACK * first : PACK * last].rearrange("p (c i j) -> p c j i", i=4, j=PACK),
+        in_=raw[:, :, first:last].rearrange("p j (c i) -> p c j i", i=4),
+    )
+
+
+def tile_picked_place_lin_bias_srt_l_kernel(tc, xT, w, b, gate, offs, out):
+    nc = tc.nc
+    mult = mybir.AluOpType.mult
+    identity = mybir.ActivationFunctionType.Identity
+
+    with ExitStack() as ctx:
+        keep = ctx.enter_context(tc.tile_pool(name="keep", bufs=1))
+        psum = ctx.enter_context(tc.psum_pool(name="psum", bufs=1))
+
+        offsets = keep.tile([P, S // 16], U16, name="offsets")
+        bias = keep.tile([P, M_TILES], F32, name="bias")
+        weight_gate = keep.tile([P, S], F32, name="weight_gate")
+        w_raw = keep.tile([P, PACK, N], F32, name="w_raw")
+        x_raw = [keep.tile([P, PACK, PIECE], F32, name=f"x_raw{c}") for c in range(PIECES)]
+        warm = keep.tile([P, 1], F32, name="warm")
+        warmed = keep.tile([P, 1], F32, name="warmed")
+
+        nc.gpsimd.memset(warm[:], 0.0)
+        nc.scalar.activation(out=warmed[:], in_=warm[:], func=identity)
+
+        xv = xT.rearrange("(p j) s -> p j s", j=PACK)
+        nc.sync.dma_start(out=x_raw[0][:], in_=xv[:, :, 0:PIECE])
+        nc.sync.dma_start(out=w_raw[:], in_=w.rearrange("(p j) m -> p j m", j=PACK))
+        nc.scalar.dma_start(out=bias[:], in_=b.rearrange("(h p) o -> p (h o)", p=P))
+        nc.sync.dma_start(offsets[:], offs)
+        nc.sync.dma_start(out=weight_gate[:, 0 : S // 2], in_=gate[0:P, 0 : S // 2])
+        nc.sync.dma_start(out=x_raw[1][:], in_=xv[:, :, PIECE : 2 * PIECE])
+        nc.sync.dma_start(out=x_raw[2][:], in_=xv[:, :, 2 * PIECE : 3 * PIECE])
+        nc.sync.dma_start(out=weight_gate[:, S // 2 : S], in_=gate[0:P, S // 2 : S])
+        nc.sync.dma_start(out=x_raw[3][:], in_=xv[:, :, 3 * PIECE : 4 * PIECE])
+
+        windows = [keep.tile([P, T], F32, name=f"window{h}") for h in range(M_TILES)]
+        for h in range(M_TILES):
+            nc.vector.memset(windows[h][:], 0.0)
+
+        w_grouped = keep.tile([P, PACK * N], BF16, name="w_grouped", align_bytes=64)
+        w_codes = keep.tile([P, N], U32, name="w_codes", align_bytes=64)
+        w_scales = keep.tile([P, N], U8, name="w_scales", align_bytes=64)
+        x_grouped = [keep.tile([P, PACK * PIECE], BF16, name=f"x_grouped{c}", align_bytes=64) for c in range(PIECES)]
+        x_codes = [keep.tile([P, PIECE], U32, name=f"x_codes{c}", align_bytes=64) for c in range(PIECES)]
+        x_scales = [keep.tile([P, PIECE], U8, name=f"x_scales{c}", align_bytes=64) for c in range(PIECES)]
+        sums = [[psum.tile([P, PIECE], F32, name=f"sums{c}_{h}") for h in range(M_TILES)] for c in range(PIECES)]
+        y = [[keep.tile([P, PIECE], F32, name=f"y{c}_{h}") for h in range(M_TILES)] for c in range(PIECES)]
+
+        vector_cols = (128, 128, 32, 64)
+
+        def group_x(c):
+            v = vector_cols[c]
+            interleave(nc.scalar.copy, x_grouped[c], x_raw[c], v, PIECE)
+            interleave(nc.vector.tensor_copy, x_grouped[c], x_raw[c], 0, v)
+
+        def quantize_x(c):
+            nc.vector.quantize_mx(out=x_codes[c][:].bitcast(FP8X4), scales=x_scales[c][:], in_=x_grouped[c][:])
+
+        def multiply(c):
+            for h in range(M_TILES):
+                cols = slice(P * h, P * (h + 1))
+                nc.tensor.matmul_mx(
+                    out=sums[c][h][:],
+                    lhsT=w_codes[:, cols].bitcast(FP8X4),
+                    lhsT_scale=w_scales[:, cols],
+                    rhs=x_codes[c][:].bitcast(FP8X4),
+                    rhs_scale=x_scales[c][:],
+                    start=True,
+                    stop=True,
+                )
+
+        def add_bias(c):
+            for h in range(M_TILES):
+                nc.scalar.activation(out=y[c][h][:], in_=sums[c][h][:], func=identity, bias=bias[:, h : h + 1])
+
+        def scatter(c, h):
+            nc.vector.tensor_tensor(
+                windows[h][:].indirect(offsets[:, LIST_COLS * c : LIST_COLS * (c + 1)]),
+                y[c][h][:],
+                weight_gate[:, PIECE * c : PIECE * (c + 1)],
+                mult,
+            )
+
+        group_x(0)
+        interleave(nc.vector.tensor_copy, w_grouped, w_raw, 0, N)
+        quantize_x(0)
+        nc.vector.quantize_mx(out=w_codes[:].bitcast(FP8X4), scales=w_scales[:], in_=w_grouped[:])
+        multiply(0)
+        group_x(1)
+        add_bias(0)
+        quantize_x(1)
+        multiply(1)
+        scatter(0, 0)
+        group_x(2)
+        add_bias(1)
+        quantize_x(2)
+        multiply(2)
+        scatter(1, 0)
+        scatter(0, 1)
+        group_x(3)
+        add_bias(2)
+        quantize_x(3)
+        multiply(3)
+        scatter(2, 0)
+        scatter(1, 1)
+        add_bias(3)
+        scatter(3, 0)
+        nc.sync.dma_start(out=out[0:P, :], in_=windows[0][:])
+        scatter(2, 1)
+        scatter(3, 1)
+        nc.sync.dma_start(out=out[P : 2 * P, :], in_=windows[1][:])

@@ -51,19 +51,28 @@ def tile_picked_place_lin_bias_srt_l_kernel(tc, xT, w, b, gate, offs, out):
         nc.scalar.activation(out=warmed[:], in_=warm[:], func=identity)
 
         xv = xT.rearrange("(p j) s -> p j s", j=PACK)
-        nc.sync.dma_start(out=x_raw[0][:], in_=xv[:, :, 0:PIECE])
+
+        def load_x(c):
+            nc.sync.dma_start(out=x_raw[c][:], in_=xv[:, :, PIECE * c : PIECE * (c + 1)])
+
+        def load_gate(first, last):
+            cols = slice(PIECE * first, PIECE * last)
+            nc.sync.dma_start(out=weight_gate[:, cols], in_=gate[0:P, cols])
+
         nc.sync.dma_start(out=w_raw[:], in_=w.rearrange("(p j) m -> p j m", j=PACK))
         nc.scalar.dma_start(out=bias[:], in_=b.rearrange("(h p) o -> p (h o)", p=P))
+        load_x(0)
+        load_gate(0, 1)
         nc.sync.dma_start(offsets[:], offs)
-        nc.sync.dma_start(out=weight_gate[:, 0 : S // 2], in_=gate[0:P, 0 : S // 2])
-        nc.sync.dma_start(out=x_raw[1][:], in_=xv[:, :, PIECE : 2 * PIECE])
-        nc.sync.dma_start(out=x_raw[2][:], in_=xv[:, :, 2 * PIECE : 3 * PIECE])
-        nc.sync.dma_start(out=weight_gate[:, S // 2 : S], in_=gate[0:P, S // 2 : S])
-        nc.sync.dma_start(out=x_raw[3][:], in_=xv[:, :, 3 * PIECE : 4 * PIECE])
+        load_x(1)
+        load_x(2)
+        load_gate(1, 2)
+        load_x(3)
+        load_gate(2, 4)
 
         windows = [keep.tile([P, T], F32, name=f"window{h}") for h in range(M_TILES)]
-        for h in range(M_TILES):
-            nc.vector.memset(windows[h][:], 0.0)
+        nc.vector.memset(windows[0][:], 0.0)
+        nc.gpsimd.memset(windows[1][:], 0.0)
 
         w_grouped = keep.tile([P, PACK * N], BF16, name="w_grouped", align_bytes=64)
         w_codes = keep.tile([P, N], U32, name="w_codes", align_bytes=64)
@@ -72,9 +81,10 @@ def tile_picked_place_lin_bias_srt_l_kernel(tc, xT, w, b, gate, offs, out):
         x_codes = [keep.tile([P, PIECE], U32, name=f"x_codes{c}", align_bytes=64) for c in range(PIECES)]
         x_scales = [keep.tile([P, PIECE], U8, name=f"x_scales{c}", align_bytes=64) for c in range(PIECES)]
         sums = [[psum.tile([P, PIECE], F32, name=f"sums{c}_{h}") for h in range(M_TILES)] for c in range(PIECES)]
-        y = [[keep.tile([P, PIECE], F32, name=f"y{c}_{h}") for h in range(M_TILES)] for c in range(PIECES)]
+        y = [keep.tile([P, S], F32, name=f"y{h}") for h in range(M_TILES)]
 
-        vector_cols = (128, 128, 32, 64)
+        vector_cols = (128, 256, 64, 0)
+        w_vector_cols = 160
 
         def group_x(c):
             v = vector_cols[c]
@@ -97,43 +107,45 @@ def tile_picked_place_lin_bias_srt_l_kernel(tc, xT, w, b, gate, offs, out):
                     stop=True,
                 )
 
-        def add_bias(c):
-            for h in range(M_TILES):
-                nc.scalar.activation(out=y[c][h][:], in_=sums[c][h][:], func=identity, bias=bias[:, h : h + 1])
+        def add_bias(c, h):
+            nc.scalar.activation(
+                out=y[h][:, PIECE * c : PIECE * (c + 1)], in_=sums[c][h][:], func=identity, bias=bias[:, h : h + 1]
+            )
 
-        def scatter(c, h):
+        def scatter(h, first, last):
             nc.vector.tensor_tensor(
-                windows[h][:].indirect(offsets[:, LIST_COLS * c : LIST_COLS * (c + 1)]),
-                y[c][h][:],
-                weight_gate[:, PIECE * c : PIECE * (c + 1)],
+                windows[h][:].indirect(offsets[:, LIST_COLS * first : LIST_COLS * last]),
+                y[h][:, PIECE * first : PIECE * last],
+                weight_gate[:, PIECE * first : PIECE * last],
                 mult,
             )
 
-        group_x(0)
-        interleave(nc.vector.tensor_copy, w_grouped, w_raw, 0, N)
-        quantize_x(0)
+        interleave(nc.vector.tensor_copy, w_grouped, w_raw, 0, w_vector_cols)
+        interleave(nc.scalar.copy, w_grouped, w_raw, w_vector_cols, N)
         nc.vector.quantize_mx(out=w_codes[:].bitcast(FP8X4), scales=w_scales[:], in_=w_grouped[:])
+        group_x(0)
+        quantize_x(0)
         multiply(0)
+        add_bias(0, 0)
         group_x(1)
-        add_bias(0)
         quantize_x(1)
         multiply(1)
-        scatter(0, 0)
+        scatter(0, 0, 1)
         group_x(2)
-        add_bias(1)
         quantize_x(2)
         multiply(2)
-        scatter(1, 0)
-        scatter(0, 1)
         group_x(3)
-        add_bias(2)
+        add_bias(1, 0)
         quantize_x(3)
         multiply(3)
-        scatter(2, 0)
-        scatter(1, 1)
-        add_bias(3)
-        scatter(3, 0)
+        scatter(0, 1, 2)
+        add_bias(2, 0)
+        scatter(0, 2, 3)
+        add_bias(3, 0)
+        scatter(0, 3, 4)
         nc.sync.dma_start(out=out[0:P, :], in_=windows[0][:])
-        scatter(2, 1)
-        scatter(3, 1)
+        for c in range(PIECES):
+            add_bias(c, 1)
+        scatter(1, 0, 1)
+        scatter(1, 1, 4)
         nc.sync.dma_start(out=out[P : 2 * P, :], in_=windows[1][:])

@@ -46,7 +46,6 @@ def tile_picked_place_lin_bias_srt_l_kernel(tc, xT, w, b, gate, offs, out):
         x_raw = [keep.tile([P, PACK, PIECE], F32, name=f"x_raw{c}") for c in range(PIECES)]
         warm = keep.tile([P, 1], F32, name="warm")
         warmed = keep.tile([P, 1], F32, name="warmed")
-
         nc.gpsimd.memset(warm[:], 0.0)
         nc.scalar.activation(out=warmed[:], in_=warm[:], func=identity)
 
@@ -59,20 +58,28 @@ def tile_picked_place_lin_bias_srt_l_kernel(tc, xT, w, b, gate, offs, out):
             cols = slice(PIECE * first, PIECE * last)
             nc.sync.dma_start(out=weight_gate[:, cols], in_=gate[0:P, cols])
 
-        nc.sync.dma_start(out=w_raw[:], in_=w.rearrange("(p j) m -> p j m", j=PACK))
-        nc.scalar.dma_start(out=bias[:], in_=b.rearrange("(h p) o -> p (h o)", p=P))
+        def load_w():
+            nc.sync.dma_start(out=w_raw[:], in_=w.rearrange("(p j) m -> p j m", j=PACK))
+
+        def load_bias(eng):
+            eng.dma_start(out=bias[:], in_=b.rearrange("(h p) o -> p (h o)", p=P))
+
+        def load_offs():
+            nc.sync.dma_start(offsets[:], offs)
+
         load_x(0)
-        load_gate(0, 1)
-        nc.sync.dma_start(offsets[:], offs)
+        load_w()
         load_x(1)
+        load_bias(nc.sync)
+        load_offs()
+        load_gate(0, 2)
         load_x(2)
-        load_gate(1, 2)
         load_x(3)
         load_gate(2, 4)
 
         windows = [keep.tile([P, T], F32, name=f"window{h}") for h in range(M_TILES)]
         nc.vector.memset(windows[0][:], 0.0)
-        nc.gpsimd.memset(windows[1][:], 0.0)
+        nc.vector.memset(windows[1][:], 0.0)
 
         w_grouped = keep.tile([P, PACK * N], BF16, name="w_grouped", align_bytes=64)
         w_codes = keep.tile([P, N], U32, name="w_codes", align_bytes=64)
@@ -80,11 +87,16 @@ def tile_picked_place_lin_bias_srt_l_kernel(tc, xT, w, b, gate, offs, out):
         x_grouped = [keep.tile([P, PACK * PIECE], BF16, name=f"x_grouped{c}", align_bytes=64) for c in range(PIECES)]
         x_codes = [keep.tile([P, PIECE], U32, name=f"x_codes{c}", align_bytes=64) for c in range(PIECES)]
         x_scales = [keep.tile([P, PIECE], U8, name=f"x_scales{c}", align_bytes=64) for c in range(PIECES)]
-        sums = [[psum.tile([P, PIECE], F32, name=f"sums{c}_{h}") for h in range(M_TILES)] for c in range(PIECES)]
         y = [keep.tile([P, S], F32, name=f"y{h}") for h in range(M_TILES)]
+        sums = {}
+        for h, segments in enumerate((((0, 1), (1, 2), (2, 3), (3, 4)), ((0, 1), (1, 2), (2, 4)))):
+            for first, last in segments:
+                bank = psum.tile([P, PIECE * (last - first)], F32, name=f"sums{h}_{first}")
+                for c in range(first, last):
+                    sums[c, h] = (bank, first, last)
 
-        vector_cols = (128, 256, 64, 0)
-        w_vector_cols = 160
+        vector_cols = (0, 160, 64, 0)
+        w_vector_cols = 128
 
         def group_x(c):
             v = vector_cols[c]
@@ -93,12 +105,11 @@ def tile_picked_place_lin_bias_srt_l_kernel(tc, xT, w, b, gate, offs, out):
 
         def quantize_x(c):
             nc.vector.quantize_mx(out=x_codes[c][:].bitcast(FP8X4), scales=x_scales[c][:], in_=x_grouped[c][:])
-
-        def multiply(c):
             for h in range(M_TILES):
                 cols = slice(P * h, P * (h + 1))
+                bank, first, last = sums[c, h]
                 nc.tensor.matmul_mx(
-                    out=sums[c][h][:],
+                    out=bank[:, PIECE * (c - first) : PIECE * (c - first + 1)],
                     lhsT=w_codes[:, cols].bitcast(FP8X4),
                     lhsT_scale=w_scales[:, cols],
                     rhs=x_codes[c][:].bitcast(FP8X4),
@@ -107,10 +118,9 @@ def tile_picked_place_lin_bias_srt_l_kernel(tc, xT, w, b, gate, offs, out):
                     stop=True,
                 )
 
-        def add_bias(c, h):
-            nc.scalar.activation(
-                out=y[h][:, PIECE * c : PIECE * (c + 1)], in_=sums[c][h][:], func=identity, bias=bias[:, h : h + 1]
-            )
+        def add_bias(h, first, last):
+            bank = sums[first, h][0]
+            nc.scalar.activation(out=y[h][:, PIECE * first : PIECE * last], in_=bank[:], func=identity, bias=bias[:, h : h + 1])
 
         def scatter(h, first, last):
             nc.vector.tensor_tensor(
@@ -120,32 +130,32 @@ def tile_picked_place_lin_bias_srt_l_kernel(tc, xT, w, b, gate, offs, out):
                 mult,
             )
 
+        def store(h):
+            nc.sync.dma_start(out=out[P * h : P * (h + 1), :], in_=windows[h][:])
+
         interleave(nc.vector.tensor_copy, w_grouped, w_raw, 0, w_vector_cols)
         interleave(nc.scalar.copy, w_grouped, w_raw, w_vector_cols, N)
         nc.vector.quantize_mx(out=w_codes[:].bitcast(FP8X4), scales=w_scales[:], in_=w_grouped[:])
         group_x(0)
         quantize_x(0)
-        multiply(0)
-        add_bias(0, 0)
+        add_bias(0, 0, 1)
         group_x(1)
         quantize_x(1)
-        multiply(1)
         scatter(0, 0, 1)
+        add_bias(0, 1, 2)
         group_x(2)
         quantize_x(2)
-        multiply(2)
-        group_x(3)
-        add_bias(1, 0)
-        quantize_x(3)
-        multiply(3)
         scatter(0, 1, 2)
-        add_bias(2, 0)
+        add_bias(0, 2, 3)
+        group_x(3)
         scatter(0, 2, 3)
-        add_bias(3, 0)
+        quantize_x(3)
+        add_bias(0, 3, 4)
         scatter(0, 3, 4)
-        nc.sync.dma_start(out=out[0:P, :], in_=windows[0][:])
-        for c in range(PIECES):
-            add_bias(c, 1)
+        store(0)
+        add_bias(1, 0, 1)
+        add_bias(1, 1, 2)
+        add_bias(1, 2, 4)
         scatter(1, 0, 1)
         scatter(1, 1, 4)
-        nc.sync.dma_start(out=out[P : 2 * P, :], in_=windows[1][:])
+        store(1)

from contextlib import ExitStack

import concourse.mybir as mybir

K, T, S, N = 512, 2048, 1024, 256
FLOPS = 2 * K * N * S
BYTES = 4 * (K * S + K * N + N + S + N * T) + 2 * 128 * (S // 16)

F32 = mybir.dt.float32
BF16 = mybir.dt.bfloat16
U32 = mybir.dt.uint32
U16 = mybir.dt.uint16
U8 = mybir.dt.uint8
FP8X4 = mybir.dt.float8_e4m3fn_x4

P = 128
PACK = 4
PIECE = 256
PIECES = S // PIECE
M_TILES = N // P
LIST_COLS = PIECE // 16


def interleave(copy, grouped, raw, first, last):
    if first == last:
        return
    copy(
        out=grouped[:, PACK * first : PACK * last].rearrange("p (c i j) -> p c j i", i=4, j=PACK),
        in_=raw[:, :, first:last].rearrange("p j (c i) -> p c j i", i=4),
    )


def tile_picked_place_lin_bias_srt_l_kernel(tc, xT, w, b, gate, offs, out):
    nc = tc.nc
    mult = mybir.AluOpType.mult
    identity = mybir.ActivationFunctionType.Identity

    with ExitStack() as ctx:
        keep = ctx.enter_context(tc.tile_pool(name="keep", bufs=1))
        psum = ctx.enter_context(tc.psum_pool(name="psum", bufs=1))

        offsets = keep.tile([P, S // 16], U16, name="offsets")
        bias = keep.tile([P, M_TILES], F32, name="bias")
        weight_gate = keep.tile([P, S], F32, name="weight_gate")
        w_raw = keep.tile([P, PACK, N], F32, name="w_raw")
        x_raw = [keep.tile([P, PACK, PIECE], F32, name=f"x_raw{c}") for c in range(PIECES)]
        warm = keep.tile([P, 1], F32, name="warm")
        warmed = keep.tile([P, 1], F32, name="warmed")
        nc.gpsimd.memset(warm[:], 0.0)
        nc.scalar.activation(out=warmed[:], in_=warm[:], func=identity)

        xv = xT.rearrange("(p j) s -> p j s", j=PACK)

        def load_x(c):
            nc.sync.dma_start(out=x_raw[c][:], in_=xv[:, :, PIECE * c : PIECE * (c + 1)])

        def load_gate(first, last):
            cols = slice(PIECE * first, PIECE * last)
            nc.sync.dma_start(out=weight_gate[:, cols], in_=gate[0:P, cols])

        def load_w():
            nc.sync.dma_start(out=w_raw[:], in_=w.rearrange("(p j) m -> p j m", j=PACK))

        def load_bias(eng):
            eng.dma_start(out=bias[:], in_=b.rearrange("(h p) o -> p (h o)", p=P))

        def load_offs():
            nc.sync.dma_start(offsets[:], offs)

        load_x(0)
        load_w()
        load_x(1)
        load_bias(nc.sync)
        load_offs()
        load_gate(0, 2)
        load_x(2)
        load_x(3)
        load_gate(2, 4)

        windows = [keep.tile([P, T], F32, name=f"window{h}") for h in range(M_TILES)]
        nc.vector.memset(windows[0][:], 0.0)
        nc.vector.memset(windows[1][:], 0.0)

        w_grouped = keep.tile([P, PACK * N], BF16, name="w_grouped", align_bytes=64)
        w_codes = keep.tile([P, N], U32, name="w_codes", align_bytes=64)
        w_scales = keep.tile([P, N], U8, name="w_scales", align_bytes=64)
        x_grouped = [keep.tile([P, PACK * PIECE], BF16, name=f"x_grouped{c}", align_bytes=64) for c in range(PIECES)]
        x_codes = [keep.tile([P, PIECE], U32, name=f"x_codes{c}", align_bytes=64) for c in range(PIECES)]
        x_scales = [keep.tile([P, PIECE], U8, name=f"x_scales{c}", align_bytes=64) for c in range(PIECES)]
        y = [keep.tile([P, S], F32, name=f"y{h}") for h in range(M_TILES)]
        sums = {}
        for h, segments in enumerate((((0, 1), (1, 2), (2, 3), (3, 4)), ((0, 1), (1, 2), (2, 4)))):
            for first, last in segments:
                bank = psum.tile([P, PIECE * (last - first)], F32, name=f"sums{h}_{first}")
                for c in range(first, last):
                    sums[c, h] = (bank, first, last)

        vector_cols = (0, 160, 64, 0)
        w_vector_cols = 128

        def group_x(c):
            v = vector_cols[c]
            interleave(nc.scalar.copy, x_grouped[c], x_raw[c], v, PIECE)
            interleave(nc.vector.tensor_copy, x_grouped[c], x_raw[c], 0, v)

        def quantize_x(c):
            nc.vector.quantize_mx(out=x_codes[c][:].bitcast(FP8X4), scales=x_scales[c][:], in_=x_grouped[c][:])
            for h in range(M_TILES):
                cols = slice(P * h, P * (h + 1))
                bank, first, last = sums[c, h]
                nc.tensor.matmul_mx(
                    out=bank[:, PIECE * (c - first) : PIECE * (c - first + 1)],
                    lhsT=w_codes[:, cols].bitcast(FP8X4),
                    lhsT_scale=w_scales[:, cols],
                    rhs=x_codes[c][:].bitcast(FP8X4),
                    rhs_scale=x_scales[c][:],
                    start=True,
                    stop=True,
                )

        def add_bias(h, first, last):
            bank = sums[first, h][0]
            nc.scalar.activation(out=y[h][:, PIECE * first : PIECE * last], in_=bank[:], func=identity, bias=bias[:, h : h + 1])

        def scatter(h, first, last):
            nc.vector.tensor_tensor(
                windows[h][:].indirect(offsets[:, LIST_COLS * first : LIST_COLS * last]),
                y[h][:, PIECE * first : PIECE * last],
                weight_gate[:, PIECE * first : PIECE * last],
                mult,
            )

        def store(h):
            nc.sync.dma_start(out=out[P * h : P * (h + 1), :], in_=windows[h][:])

        interleave(nc.vector.tensor_copy, w_grouped, w_raw, 0, w_vector_cols)
        interleave(nc.scalar.copy, w_grouped, w_raw, w_vector_cols, N)
        nc.vector.quantize_mx(out=w_codes[:].bitcast(FP8X4), scales=w_scales[:], in_=w_grouped[:])
        group_x(0)
        quantize_x(0)
        add_bias(0, 0, 1)
        group_x(1)
        quantize_x(1)
        scatter(0, 0, 1)
        add_bias(0, 1, 2)
        group_x(2)
        quantize_x(2)
        scatter(0, 1, 2)
        add_bias(0, 2, 3)
        group_x(3)
        scatter(0, 2, 3)
        quantize_x(3)
        add_bias(0, 3, 4)
        scatter(0, 3, 4)
        store(0)
        add_bias(1, 0, 1)
        add_bias(1, 1, 2)
        add_bias(1, 2, 4)
        scatter(1, 0, 1)
        scatter(1, 1, 4)
        store(1)
